import numpy as np
import ml_dtypes


def mxq(x, axis, fmt="e4m3"):
    dtype, down = {"e4m3": (ml_dtypes.float8_e4m3fn, 7), "e5m2": (ml_dtypes.float8_e5m2, 14)}[fmt]
    v = np.moveaxis(np.asarray(x, np.float32).astype(ml_dtypes.bfloat16).astype(np.float64), axis, -1)
    blocks = v.reshape(v.shape[:-1] + (-1, 32))
    amax = np.abs(blocks).max(-1, keepdims=True)
    byte = np.maximum(np.where(amax > 0, np.frexp(amax)[1] - 1 + 127, 0) - down, 1)
    scale = np.exp2(byte - 127.0)
    codes = (blocks / scale).astype(np.float32).astype(dtype).astype(np.float64)
    return np.moveaxis((codes * scale).reshape(v.shape), -1, axis)


WIDE = False


def mx_kscale(k):
    if not WIDE:
        return np.ones(k)
    levels = np.array([10, -10, 5, -5, 0])
    if k % 512:
        return np.exp2(np.random.permutation(np.resize(levels, k // 32))).repeat(32)
    a = np.empty((k // 512, 16))
    for p in range(k // 512):
        a[p, :8] = np.random.permutation(np.resize(levels, 8))
        for g in range(8):
            far = levels[np.abs(levels - a[p, g]) >= 10]
            a[p, g + 8] = far[np.random.randint(len(far))]
    return np.exp2(a.ravel()).repeat(32)


def f64(x):
    return np.asarray(x).astype(np.float64)


def striped(idx):
    return np.tile(idx.reshape(-1, 16).T, (8, 1)).astype(np.uint16)


def unstriped(offs):
    return offs[:16].T.reshape(-1).astype(np.int64)


def striped8(idx):
    return np.concatenate([x.reshape(-1, 16).T for x in idx]).astype(np.uint16)


def runs(offs, k):
    lists = np.stack([offs[16 * r : 16 * r + 16].T.reshape(-1) for r in range(8)]).astype(np.int64)
    return lists[np.arange(k) % 512 // 64]


def pack_weight(w):
    k, n = w.shape
    w = f64(np.asarray(w, np.float32).astype(ml_dtypes.bfloat16)).reshape(k // 32, 32, n)
    amax = np.abs(w).max(1)
    byte = np.clip(np.where(amax > 0, np.frexp(amax)[1] - 1 + 127 - 7, 1), 1, 254)
    scaled = (w * np.exp2(127.0 - byte)[:, None, :]).reshape(k, n).astype(np.float32)
    words = np.ascontiguousarray(scaled.reshape(k // 512, 128, 4, n).transpose(0, 1, 3, 2)).astype(ml_dtypes.float8_e4m3fn).view(np.uint8)
    return words, np.ascontiguousarray(byte.astype(np.uint8).reshape(k // 512, 16, n))


def unpack_weight(words, scales):
    g, p, n, _ = words.shape
    vals = np.ascontiguousarray(words).view(ml_dtypes.float8_e4m3fn).astype(np.float64) * np.repeat(np.exp2(scales.astype(np.float64) - 127.0), 8, axis=1)[..., None]
    return vals.transpose(0, 1, 3, 2).reshape(g * 512, n)


def relu(v):
    return np.maximum(v, 0.0)


K, T, S, G, H, C = 512, 1024, 512, 2048, 512, 512


def setup_inputs():
    n = np.random.standard_normal
    s = mx_kscale(K)[:, None]
    packed_xT = pack_weight(n((K, T)) * s)
    packed_dT = pack_weight(n((K, G)) / s)
    return {
        "x_words": packed_xT[0],
        "x_scales": packed_xT[1],
        "d_words": packed_dT[0],
        "d_scales": packed_dT[1],
        "gs": (np.random.uniform(0.5, 1.5, (K, 1)) / s).astype(np.float32),
        "offs": striped(np.random.permutation(T)[:S]),
        "k1": striped8(np.random.randint(0, G, (8, H))),
        "n1": striped8(np.stack([np.random.permutation(S) for _ in range(8)])),
        "n2": striped8(np.stack([np.random.permutation(S) for _ in range(8)])),
        "cand": striped(np.random.permutation(T)[:C]),
        "n3": striped8(np.stack([np.random.permutation(S) for _ in range(8)])),
        "n4": striped8(np.stack([np.random.permutation(S) for _ in range(8)])),
    }


def reference(x_words, x_scales, d_words, d_scales, gs, offs, k1, n1, n2, cand, n3, n4):
    x_cand = unpack_weight(x_words, x_scales)[:, unstriped(cand)]
    d_k1 = unpack_weight(d_words, d_scales)[np.arange(K)[:, None], runs(k1, K)]
    xq = unpack_weight(x_words, x_scales)[:, unstriped(offs)]
    h = 0.0625 * (d_k1.T @ xq)
    pa = h - (h[np.arange(H)[:, None], runs(n1, H)])
    pb = h[np.arange(H)[:, None], runs(n2, H)] - h
    z = f64(gs) * (relu(np.minimum(pa, pb)) - (relu(-1.0 * np.maximum(pa, pb))))
    s = 0.0625 * ((x_cand.T @ mxq(z, 0, "e4m3")))
    return 0.75 * (s[np.arange(C)[:, None], runs(n3, C)] + s[np.arange(C)[:, None], runs(n4, C)]) - s

@@ -1,0 +1,184 @@
+from contextlib import ExitStack
+
+import concourse.mybir as mybir
+
+K, T, S, G, H, C = 512, 1024, 512, 2048, 512, 512
+FLOPS = 2 * K * H * S + 2 * H * C * S
+
+F32 = mybir.dt.float32
+BF16 = mybir.dt.bfloat16
+I32 = mybir.dt.int32
+U32 = mybir.dt.uint32
+U16 = mybir.dt.uint16
+U8 = mybir.dt.uint8
+FP8X4 = mybir.dt.float8_e4m3fn_x4
+ALU = mybir.AluOpType
+COPY = mybir.ActivationFunctionType.Copy
+
+P = 128
+PACK = 4
+GROUP = 16
+Z_CHUNKS = ((0, 256), (256, 384), (384, 512))
+OUT_CHUNKS = ((0, 256), (256, 512))
+
+
+def entries(lst, lo, hi):
+    return lst[:, lo // GROUP : hi // GROUP]
+
+
+def deal(nc, dst, src, run):
+    nc.vector.tensor_copy(
+        out=dst.rearrange("p (t c i) -> p c t i", t=PACK, i=run),
+        in_=src.rearrange("p (c i t) -> p c t i", t=PACK, i=run),
+    )
+
+
+def place_scale_rows(queues, dst, src):
+    for q in range(4):
+        queues[q % len(queues)].dma_start(
+            out=dst[32 * q : 32 * q + 4, :].bitcast(I32),
+            in_=src[32 * q : 32 * q + 32 : 8, :].bitcast(I32),
+        )
+
+
+def interleave(nc, dst, src):
+    nc.scalar.copy(
+        out=dst[:].rearrange("p (c i) t -> p c t i", i=4),
+        in_=src[:].rearrange("p t (c i) -> p c t i", i=4),
+    )
+
+
+def tile_picked_pqcminmodlap_none_p_kernel(tc, x_words, x_scales, d_words, d_scales, gs, offs, k1, n1, n2, cand, n3, n4, out):
+    nc = tc.nc
+    with ExitStack() as ctx:
+        keep = ctx.enter_context(tc.tile_pool(name="keep", bufs=1))
+        psum = ctx.enter_context(tc.psum_pool(name="psum", bufs=1))
+
+        def load_list(name, src):
+            tile = keep.tile([P, S // GROUP], U16, name=name)
+            nc.sync.dma_start(tile[:], src)
+            return tile
+
+        d_byte_table = keep.tile([P, G], U8)
+        x_byte_table = keep.tile([P, T], U8)
+        nc.vector.memset(d_byte_table[:].bitcast(I32), 0)
+        nc.vector.memset(x_byte_table[:].bitcast(I32), 0)
+        first_scales = keep.tile([P, H + S], U8, align_bytes=64)
+        cand_scales = keep.tile([P, C], U8, align_bytes=64)
+        nc.vector.memset(first_scales[:].bitcast(I32), 0)
+        nc.vector.memset(cand_scales[:].bitcast(I32), 0)
+        k1_list = load_list("k1_list", k1)
+        offs_list = load_list("offs_list", offs)
+        gain = keep.tile([P, PACK], F32)
+        nc.sync.dma_start(out=gain[:], in_=gs.rearrange("(p t) o -> p (t o)", t=PACK))
+        cand_list = load_list("cand_list", cand)
+        nc.sync.dma_start(out=d_byte_table[0:P:8, :].bitcast(I32), in_=d_scales[0].bitcast(I32))
+        nc.sync.dma_start(out=x_byte_table[0:P:8, :].bitcast(I32), in_=x_scales[0].bitcast(I32))
+        x_word_table = keep.tile([P, T], I32)
+        d_word_table = keep.tile([P, G], I32)
+        nc.sync.dma_start(out=x_word_table[:], in_=x_words[0].rearrange("p n t -> p (n t)").bitcast(I32))
+        nc.sync.dma_start(out=d_word_table[:], in_=d_words[0].rearrange("p n t -> p (n t)").bitcast(I32))
+        n1_list = load_list("n1_list", n1)
+        n2_list = load_list("n2_list", n2)
+        n3_list = load_list("n3_list", n3)
+        n4_list = load_list("n4_list", n4)
+
+        gain_pos = keep.tile([P, PACK], F32)
+        gain_neg = keep.tile([P, PACK], F32)
+        nc.scalar.activation(gain_pos[:], gain[:], COPY, scale=0.0625)
+        nc.scalar.activation(gain_neg[:], gain[:], COPY, scale=-0.0625)
+
+        first_bytes = keep.tile([P, H + S], U8, tag="picked_bytes")
+        nc.vector.tensor_copy(first_bytes[:, 0:H], d_byte_table[:].indirect(k1_list[:]))
+        nc.vector.tensor_copy(first_bytes[:, H:], x_byte_table[:].indirect(offs_list[:]))
+        place_scale_rows((nc.sync,), first_scales, first_bytes)
+
+        xq_words = keep.tile([P, S], U32, align_bytes=64)
+        nc.vector.tensor_copy(xq_words[:], x_word_table[:].bitcast(U32).indirect(offs_list[:]))
+        dq_picked = keep.tile([P, H], U32, tag="picked_words")
+        nc.vector.tensor_copy(dq_picked[:], d_word_table[:].bitcast(U32).indirect(k1_list[:]))
+        dq_words = keep.tile([P, H], U32, align_bytes=64)
+        dq_scales = keep.tile([P, H], U8, align_bytes=64)
+        deal(nc, dq_scales[:], first_scales[:, 0:H], 16)
+        deal(nc, dq_words[:], dq_picked[:], 4)
+
+        h_pos, h_neg = [], []
+        for t in range(PACK):
+            rows = slice(t * P, (t + 1) * P)
+            bank = psum.tile([P, S], F32, name=f"h_bank{t}")
+            nc.tensor.matmul_mx(out=bank[:], lhsT=dq_words[:, rows].bitcast(FP8X4), lhsT_scale=dq_scales[:, rows],
+                                rhs=xq_words[:].bitcast(FP8X4), rhs_scale=first_scales[:, H:], start=True, stop=True)
+            pos = keep.tile([P, S], F32, name=f"h_pos{t}")
+            neg = keep.tile([P, S], F32, name=f"h_neg{t}")
+            nc.scalar.activation(neg[:], bank[:], COPY, scale=gain_neg[:, t : t + 1])
+            nc.scalar.activation(pos[:], bank[:], COPY, scale=gain_pos[:, t : t + 1])
+            h_pos.append(pos)
+            h_neg.append(neg)
+
+        cand_bytes = keep.tile([P, C], U8, tag="picked_bytes")
+        cand_dealt = keep.tile([P, C], U8)
+        cand_picked = keep.tile([P, C], U32, tag="picked_words")
+        cand_words = keep.tile([P, C], U32, align_bytes=64)
+        nc.vector.tensor_copy(cand_bytes[:], x_byte_table[:].indirect(cand_list[:]))
+        nc.vector.tensor_copy(cand_picked[:], x_word_table[:].bitcast(U32).indirect(cand_list[:]))
+        deal(nc, cand_dealt[:], cand_bytes[:], 16)
+        deal(nc, cand_words[:], cand_picked[:], 4)
+        place_scale_rows((nc.sync,), cand_scales, cand_dealt)
+
+        s_banks = [psum.tile([P, S], F32, name=f"s_bank{t}") for t in range(PACK)]
+        s_pos = [keep.tile([P, S], F32, name=f"s_pos{t}") for t in range(PACK)]
+        s_neg = [keep.tile([P, S], F32, name=f"s_neg{t}") for t in range(PACK)]
+
+        def differences(lo, hi):
+            n = hi - lo
+            pa = keep.tile([P, PACK, n], F32, name=f"pa{lo}")
+            pb = keep.tile([P, PACK, n], F32, name=f"pb{lo}")
+            for t in range(PACK):
+                nc.vector.tensor_tensor(pa[:, t, :], h_neg[t][:].indirect(entries(n1_list, lo, hi)), h_pos[t][:, lo:hi], ALU.add)
+                nc.vector.tensor_tensor(pb[:, t, :], h_pos[t][:].indirect(entries(n2_list, lo, hi)), h_neg[t][:, lo:hi], ALU.add)
+            pa16 = keep.tile([P, n, PACK], BF16, name=f"pa16_{lo}")
+            pb16 = keep.tile([P, n, PACK], BF16, name=f"pb16_{lo}")
+            interleave(nc, pa16, pa)
+            interleave(nc, pb16, pb)
+            return pa16[:].rearrange("p n t -> p (n t)"), pb16[:].rearrange("p n t -> p (n t)")
+
+        def score(lo, hi, pa16, pb16):
+            n = hi - lo
+            upper = keep.tile([P, PACK * n], BF16, name=f"upper{lo}")
+            lower = keep.tile([P, PACK * n], BF16, name=f"lower{lo}")
+            capped = keep.tile([P, PACK * n], BF16, name=f"capped{lo}")
+            z = keep.tile([P, PACK * n], BF16, name=f"z{lo}", align_bytes=64)
+            z_words = keep.tile([P, n], U32, name=f"z_words{lo}", align_bytes=64)
+            z_scales = keep.tile([P, n], U8, name=f"z_scales{lo}", align_bytes=64)
+            nc.vector.tensor_scalar(upper[:], pb16, 0.0, None, ALU.max)
+            nc.vector.tensor_scalar(lower[:], pb16, 0.0, None, ALU.min)
+            nc.vector.tensor_tensor(capped[:], pa16, upper[:], ALU.min)
+            nc.vector.tensor_tensor(z[:], capped[:], lower[:], ALU.max)
+            nc.vector.quantize_mx(out=z_words[:].bitcast(FP8X4), scales=z_scales[:], in_=z[:])
+            for t in range(PACK):
+                rows = slice(t * P, (t + 1) * P)
+                nc.tensor.matmul_mx(out=s_banks[t][:, lo:hi], lhsT=cand_words[:, rows].bitcast(FP8X4), lhsT_scale=cand_scales[:, rows],
+                                    rhs=z_words[:].bitcast(FP8X4), rhs_scale=z_scales[:], start=True, stop=True)
+            nc.scalar.activation(s_pos[0][:, lo:hi], s_banks[0][:, lo:hi], COPY, scale=0.75 * 0.0625)
+            nc.scalar.activation(s_neg[0][:, lo:hi], s_banks[0][:, lo:hi], COPY, scale=-0.0625)
+
+        pending = None
+        for lo, hi in Z_CHUNKS:
+            rounded = differences(lo, hi)
+            if pending is not None:
+                score(*pending)
+            pending = (lo, hi) + rounded
+        score(*pending)
+
+        out_rows = out.rearrange("(p t) j -> p t j", t=PACK)
+        for t in range(PACK):
+            if t > 0:
+                nc.scalar.activation(s_pos[t][:], s_banks[t][:], COPY, scale=0.75 * 0.0625)
+                nc.scalar.activation(s_neg[t][:], s_banks[t][:], COPY, scale=-0.0625)
+            part = keep.tile([P, S], F32, name=f"part{t}")
+            res = keep.tile([P, S], F32, name=f"res{t}")
+            for lo, hi in OUT_CHUNKS:
+                nc.vector.tensor_tensor(part[:, lo:hi], s_pos[t][:].indirect(entries(n3_list, lo, hi)), s_neg[t][:, lo:hi], ALU.add)
+            for lo, hi in OUT_CHUNKS:
+                nc.vector.tensor_tensor(res[:, lo:hi], s_pos[t][:].indirect(entries(n4_list, lo, hi)), part[:, lo:hi], ALU.add)
+                nc.sync.dma_start(out=out_rows[:, t, lo:hi], in_=res[:, lo:hi])

@@ -18,8 +18,10 @@ COPY = mybir.ActivationFunctionType.Copy
 P = 128
 PACK = 4
 GROUP = 16
-Z_CHUNKS = ((0, 256), (256, 384), (384, 512))
-OUT_CHUNKS = ((0, 256), (256, 512))
+HALVES = ((0, 256), (256, 512))
+WHOLE = ((0, 512),)
+PB_AT = (4096, 8192)
+QUARTER = 128
 
 
 def entries(lst, lo, hi):
@@ -41,10 +43,12 @@ def place_scale_rows(queues, dst, src):
         )
 
 
-def interleave(nc, dst, src):
-    nc.scalar.copy(
-        out=dst[:].rearrange("p (c i) t -> p c t i", i=4),
-        in_=src[:].rearrange("p t (c i) -> p c t i", i=4),
+def interleave(nc, dst, src, sign):
+    nc.scalar.activation(
+        dst.rearrange("p (c i) t -> p c t i", i=4),
+        src.rearrange("p t (c i) -> p c t i", i=4),
+        COPY,
+        scale=sign,
     )
 
 
@@ -52,6 +56,7 @@ def tile_picked_pqcminmodlap_none_p_kernel(tc, x_words, x_scales, d_words, d_sca
     nc = tc.nc
     with ExitStack() as ctx:
         keep = ctx.enter_context(tc.tile_pool(name="keep", bufs=1))
+        reuse = ctx.enter_context(tc.tile_pool(name="reuse", bufs=1))
         psum = ctx.enter_context(tc.psum_pool(name="psum", bufs=1))
 
         def load_list(name, src):
@@ -69,116 +74,123 @@ def tile_picked_pqcminmodlap_none_p_kernel(tc, x_words, x_scales, d_words, d_sca
         nc.vector.memset(cand_scales[:].bitcast(I32), 0)
         k1_list = load_list("k1_list", k1)
         offs_list = load_list("offs_list", offs)
-        gain = keep.tile([P, PACK], F32)
-        nc.sync.dma_start(out=gain[:], in_=gs.rearrange("(p t) o -> p (t o)", t=PACK))
+        gains = reuse.tile([P, 16], F32, offset=PB_AT[1] - 32)
+        gain, h_gain = gains[:, 0:PACK], gains[:, 8 : 8 + PACK]
+        nc.gpsimd.dma_start(out=gain, in_=gs.rearrange("(p t) o -> p (t o)", t=PACK))
         cand_list = load_list("cand_list", cand)
+        n1_list = load_list("n1_list", n1)
         nc.sync.dma_start(out=d_byte_table[0:P:8, :].bitcast(I32), in_=d_scales[0].bitcast(I32))
         nc.sync.dma_start(out=x_byte_table[0:P:8, :].bitcast(I32), in_=x_scales[0].bitcast(I32))
         x_word_table = keep.tile([P, T], I32)
         d_word_table = keep.tile([P, G], I32)
         nc.sync.dma_start(out=x_word_table[:], in_=x_words[0].rearrange("p n t -> p (n t)").bitcast(I32))
         nc.sync.dma_start(out=d_word_table[:], in_=d_words[0].rearrange("p n t -> p (n t)").bitcast(I32))
-        n1_list = load_list("n1_list", n1)
         n2_list = load_list("n2_list", n2)
         n3_list = load_list("n3_list", n3)
         n4_list = load_list("n4_list", n4)
 
-        gain_pos = keep.tile([P, PACK], F32)
-        gain_neg = keep.tile([P, PACK], F32)
-        nc.scalar.activation(gain_pos[:], gain[:], COPY, scale=0.0625)
-        nc.scalar.activation(gain_neg[:], gain[:], COPY, scale=-0.0625)
+        nc.scalar.activation(h_gain, gain, COPY, scale=0.0625)
 
-        first_bytes = keep.tile([P, H + S], U8, tag="picked_bytes")
+        first_bytes = reuse.tile([P, H + S], U8, offset=0)
         nc.vector.tensor_copy(first_bytes[:, 0:H], d_byte_table[:].indirect(k1_list[:]))
         nc.vector.tensor_copy(first_bytes[:, H:], x_byte_table[:].indirect(offs_list[:]))
         place_scale_rows((nc.sync,), first_scales, first_bytes)
 
         xq_words = keep.tile([P, S], U32, align_bytes=64)
         nc.vector.tensor_copy(xq_words[:], x_word_table[:].bitcast(U32).indirect(offs_list[:]))
-        dq_picked = keep.tile([P, H], U32, tag="picked_words")
+        dq_picked = keep.tile([P, H], U32)
         nc.vector.tensor_copy(dq_picked[:], d_word_table[:].bitcast(U32).indirect(k1_list[:]))
         dq_words = keep.tile([P, H], U32, align_bytes=64)
         dq_scales = keep.tile([P, H], U8, align_bytes=64)
         deal(nc, dq_scales[:], first_scales[:, 0:H], 16)
         deal(nc, dq_words[:], dq_picked[:], 4)
 
-        h_pos, h_neg = [], []
+        windows = [keep.tile([P, S if t == 0 else 2 * S], F32, name=f"window{t}") for t in range(PACK)]
+        h_last = keep.tile([P, S], F32)
+        h_plain = [windows[t][:, S:] for t in range(1, PACK)] + [h_last[:]]
         for t in range(PACK):
             rows = slice(t * P, (t + 1) * P)
-            bank = psum.tile([P, S], F32, name=f"h_bank{t}")
+            bank = psum.tile([P, S], F32, name=f"h_bank{t}", tag=f"bank{PACK + t}")
             nc.tensor.matmul_mx(out=bank[:], lhsT=dq_words[:, rows].bitcast(FP8X4), lhsT_scale=dq_scales[:, rows],
                                 rhs=xq_words[:].bitcast(FP8X4), rhs_scale=first_scales[:, H:], start=True, stop=True)
-            pos = keep.tile([P, S], F32, name=f"h_pos{t}")
-            neg = keep.tile([P, S], F32, name=f"h_neg{t}")
-            nc.scalar.activation(neg[:], bank[:], COPY, scale=gain_neg[:, t : t + 1])
-            nc.scalar.activation(pos[:], bank[:], COPY, scale=gain_pos[:, t : t + 1])
-            h_pos.append(pos)
-            h_neg.append(neg)
+            nc.scalar.activation(windows[t][:, 0:S], bank[:], COPY, scale=h_gain[:, t : t + 1])
+            nc.scalar.activation(h_plain[t], bank[:], COPY, scale=h_gain[:, t : t + 1])
 
-        cand_bytes = keep.tile([P, C], U8, tag="picked_bytes")
+        cand_bytes = reuse.tile([P, C], U8, offset=0)
         cand_dealt = keep.tile([P, C], U8)
-        cand_picked = keep.tile([P, C], U32, tag="picked_words")
-        cand_words = keep.tile([P, C], U32, align_bytes=64)
+        cand_words = reuse.tile([P, C], U32, align_bytes=64, offset=C)
         nc.vector.tensor_copy(cand_bytes[:], x_byte_table[:].indirect(cand_list[:]))
-        nc.vector.tensor_copy(cand_picked[:], x_word_table[:].bitcast(U32).indirect(cand_list[:]))
+        nc.vector.tensor_copy(cand_words[:].rearrange("p (t m) -> p m t", t=PACK), x_word_table[:].bitcast(U32).indirect(cand_list[:]))
         deal(nc, cand_dealt[:], cand_bytes[:], 16)
-        deal(nc, cand_words[:], cand_picked[:], 4)
         place_scale_rows((nc.sync,), cand_scales, cand_dealt)
 
-        s_banks = [psum.tile([P, S], F32, name=f"s_bank{t}") for t in range(PACK)]
-        s_pos = [keep.tile([P, S], F32, name=f"s_pos{t}") for t in range(PACK)]
-        s_neg = [keep.tile([P, S], F32, name=f"s_neg{t}") for t in range(PACK)]
-
-        def differences(lo, hi):
-            n = hi - lo
-            pa = keep.tile([P, PACK, n], F32, name=f"pa{lo}")
-            pb = keep.tile([P, PACK, n], F32, name=f"pb{lo}")
+        minus_pa = keep.tile([P, PACK, S], F32)
+        for t in range(PACK):
+            for lo, hi in HALVES if t == 0 else WHOLE:
+                nc.vector.tensor_tensor(minus_pa[:, t, lo:hi], windows[t][:].indirect(entries(n1_list, lo, hi)), h_plain[t][:, lo:hi], ALU.subtract)
+        pa16, pb16 = [], []
+        for lo, hi in HALVES:
+            tile = keep.tile([P, hi - lo, PACK], BF16, name=f"pa16_{lo}")
+            interleave(nc, tile[:], minus_pa[:, :, lo:hi], -1.0)
+            pa16.append(tile[:].rearrange("p n t -> p (n t)"))
+        for (lo, hi), at in zip(HALVES, PB_AT):
+            pb = reuse.tile([P, PACK, hi - lo], F32, name=f"pb{lo}", offset=at)
             for t in range(PACK):
-                nc.vector.tensor_tensor(pa[:, t, :], h_neg[t][:].indirect(entries(n1_list, lo, hi)), h_pos[t][:, lo:hi], ALU.add)
-                nc.vector.tensor_tensor(pb[:, t, :], h_pos[t][:].indirect(entries(n2_list, lo, hi)), h_neg[t][:, lo:hi], ALU.add)
-            pa16 = keep.tile([P, n, PACK], BF16, name=f"pa16_{lo}")
-            pb16 = keep.tile([P, n, PACK], BF16, name=f"pb16_{lo}")
-            interleave(nc, pa16, pa)
-            interleave(nc, pb16, pb)
-            return pa16[:].rearrange("p n t -> p (n t)"), pb16[:].rearrange("p n t -> p (n t)")
+                nc.vector.tensor_tensor(pb[:, t, :], windows[t][:].indirect(entries(n2_list, lo, hi)), h_plain[t][:, lo:hi], ALU.subtract)
+            tile = keep.tile([P, hi - lo, PACK], BF16, name=f"pb16_{lo}")
+            interleave(nc, tile[:], pb[:], 1.0)
+            pb16.append(tile[:].rearrange("p n t -> p (n t)"))
 
-        def score(lo, hi, pa16, pb16):
-            n = hi - lo
-            upper = keep.tile([P, PACK * n], BF16, name=f"upper{lo}")
-            lower = keep.tile([P, PACK * n], BF16, name=f"lower{lo}")
-            capped = keep.tile([P, PACK * n], BF16, name=f"capped{lo}")
-            z = keep.tile([P, PACK * n], BF16, name=f"z{lo}", align_bytes=64)
-            z_words = keep.tile([P, n], U32, name=f"z_words{lo}", align_bytes=64)
-            z_scales = keep.tile([P, n], U8, name=f"z_scales{lo}", align_bytes=64)
-            nc.vector.tensor_scalar(upper[:], pb16, 0.0, None, ALU.max)
-            nc.vector.tensor_scalar(lower[:], pb16, 0.0, None, ALU.min)
-            nc.vector.tensor_tensor(capped[:], pa16, upper[:], ALU.min)
-            nc.vector.tensor_tensor(z[:], capped[:], lower[:], ALU.max)
-            nc.vector.quantize_mx(out=z_words[:].bitcast(FP8X4), scales=z_scales[:], in_=z[:])
-            for t in range(PACK):
-                rows = slice(t * P, (t + 1) * P)
-                nc.tensor.matmul_mx(out=s_banks[t][:, lo:hi], lhsT=cand_words[:, rows].bitcast(FP8X4), lhsT_scale=cand_scales[:, rows],
-                                    rhs=z_words[:].bitcast(FP8X4), rhs_scale=z_scales[:], start=True, stop=True)
-            nc.scalar.activation(s_pos[0][:, lo:hi], s_banks[0][:, lo:hi], COPY, scale=0.75 * 0.0625)
-            nc.scalar.activation(s_neg[0][:, lo:hi], s_banks[0][:, lo:hi], COPY, scale=-0.0625)
-
-        pending = None
-        for lo, hi in Z_CHUNKS:
-            rounded = differences(lo, hi)
-            if pending is not None:
-                score(*pending)
-            pending = (lo, hi) + rounded
-        score(*pending)
+        s_plain = [keep.tile([P, S], F32, name=f"s_plain{t}") for t in range(PACK)]
+        last_bank = psum.tile([P, S], F32)
+        for half, (lo, hi) in enumerate(HALVES):
+            n = PACK * (hi - lo)
+            s_banks = [psum.tile([P, hi - lo], F32, name=f"s_bank{half}_{t}", tag=f"bank{PACK * half + t}")[:] for t in range(PACK - 1)]
+            s_banks.append(last_bank[:, lo:hi])
+            upper = keep.tile([P, n], BF16, name=f"upper{lo}")
+            lower = keep.tile([P, n], BF16, name=f"lower{lo}")
+            capped = keep.tile([P, n], BF16, name=f"capped{lo}")
+            z = keep.tile([P, n], BF16, name=f"z{lo}", align_bytes=64)
+            nc.vector.tensor_scalar(upper[:], pb16[half], 0.0, None, ALU.max)
+            nc.vector.tensor_scalar(lower[:], pb16[half], 0.0, None, ALU.min)
+            parts = [slice(PACK * c, PACK * (c + QUARTER)) for c in range(0, hi - lo, QUARTER)]
+            for part in parts:
+                nc.vector.tensor_tensor(capped[:, part], pa16[half][:, part], upper[:, part], ALU.min)
+            for part in parts:
+                nc.vector.tensor_tensor(z[:, part], capped[:, part], lower[:, part], ALU.max)
+            for k, part in enumerate(parts):
+                cols = slice(lo + k * QUARTER, lo + (k + 1) * QUARTER)
+                z_words = keep.tile([P, QUARTER], U32, name=f"z_words{cols.start}", align_bytes=64)
+                z_scales = keep.tile([P, QUARTER], U8, name=f"z_scales{cols.start}", align_bytes=64)
+                nc.vector.quantize_mx(out=z_words[:].bitcast(FP8X4), scales=z_scales[:], in_=z[:, part])
+                for t in range(PACK):
+                    rows = slice(t * P, (t + 1) * P)
+                    nc.tensor.matmul_mx(out=s_banks[t][:, k * QUARTER : (k + 1) * QUARTER], lhsT=cand_words[:, rows].bitcast(FP8X4), lhsT_scale=cand_scales[:, rows],
+                                        rhs=z_words[:].bitcast(FP8X4), rhs_scale=z_scales[:], start=True, stop=True)
+            for t in range(PACK - 1):
+                nc.scalar.activation(windows[t][:, lo:hi], s_banks[t], COPY, scale=0.75 * 0.0625)
+                nc.scalar.activation(s_plain[t][:, lo:hi], s_banks[t], COPY, scale=-0.0625)
+        nc.scalar.activation(windows[PACK - 1][:, 0:S], last_bank[:], COPY, scale=0.75 * 0.0625)
+        nc.scalar.activation(s_plain[PACK - 1][:], last_bank[:], COPY, scale=-0.0625)
 
         out_rows = out.rearrange("(p t) j -> p t j", t=PACK)
-        for t in range(PACK):
-            if t > 0:
-                nc.scalar.activation(s_pos[t][:], s_banks[t][:], COPY, scale=0.75 * 0.0625)
-                nc.scalar.activation(s_neg[t][:], s_banks[t][:], COPY, scale=-0.0625)
+
+        def first_lookup(t):
             part = keep.tile([P, S], F32, name=f"part{t}")
+            for lo, hi in HALVES if t == 0 else WHOLE:
+                nc.vector.tensor_tensor(part[:, lo:hi], windows[t][:].indirect(entries(n3_list, lo, hi)), s_plain[t][:, lo:hi], ALU.add)
+            return part
+
+        def second_lookup(t, part):
             res = keep.tile([P, S], F32, name=f"res{t}")
-            for lo, hi in OUT_CHUNKS:
-                nc.vector.tensor_tensor(part[:, lo:hi], s_pos[t][:].indirect(entries(n3_list, lo, hi)), s_neg[t][:, lo:hi], ALU.add)
-            for lo, hi in OUT_CHUNKS:
-                nc.vector.tensor_tensor(res[:, lo:hi], s_pos[t][:].indirect(entries(n4_list, lo, hi)), part[:, lo:hi], ALU.add)
+            for lo, hi in HALVES if t in (0, PACK - 1) else WHOLE:
+                nc.vector.tensor_tensor(res[:, lo:hi], windows[t][:].indirect(entries(n4_list, lo, hi)), part[:, lo:hi], ALU.add)
                 nc.sync.dma_start(out=out_rows[:, t, lo:hi], in_=res[:, lo:hi])
+
+        second_lookup(0, first_lookup(0))
+        part = first_lookup(1)
+        for t in range(1, PACK - 1):
+            ahead = first_lookup(t + 1)
+            second_lookup(t, part)
+            part = ahead
+        second_lookup(PACK - 1, part)

from contextlib import ExitStack

import concourse.mybir as mybir

K, T, S, G, H, C = 512, 1024, 512, 2048, 512, 512
FLOPS = 2 * K * H * S + 2 * H * C * S

F32 = mybir.dt.float32
BF16 = mybir.dt.bfloat16
I32 = mybir.dt.int32
U32 = mybir.dt.uint32
U16 = mybir.dt.uint16
U8 = mybir.dt.uint8
FP8X4 = mybir.dt.float8_e4m3fn_x4
ALU = mybir.AluOpType
COPY = mybir.ActivationFunctionType.Copy

P = 128
PACK = 4
GROUP = 16
HALVES = ((0, 256), (256, 512))
WHOLE = ((0, 512),)
PB_AT = (4096, 8192)
QUARTER = 128


def entries(lst, lo, hi):
    return lst[:, lo // GROUP : hi // GROUP]


def deal(nc, dst, src, run):
    nc.vector.tensor_copy(
        out=dst.rearrange("p (t c i) -> p c t i", t=PACK, i=run),
        in_=src.rearrange("p (c i t) -> p c t i", t=PACK, i=run),
    )


def place_scale_rows(queues, dst, src):
    for q in range(4):
        queues[q % len(queues)].dma_start(
            out=dst[32 * q : 32 * q + 4, :].bitcast(I32),
            in_=src[32 * q : 32 * q + 32 : 8, :].bitcast(I32),
        )


def interleave(nc, dst, src, sign):
    nc.scalar.activation(
        dst.rearrange("p (c i) t -> p c t i", i=4),
        src.rearrange("p t (c i) -> p c t i", i=4),
        COPY,
        scale=sign,
    )


def tile_picked_pqcminmodlap_none_p_kernel(tc, x_words, x_scales, d_words, d_scales, gs, offs, k1, n1, n2, cand, n3, n4, out):
    nc = tc.nc
    with ExitStack() as ctx:
        keep = ctx.enter_context(tc.tile_pool(name="keep", bufs=1))
        reuse = ctx.enter_context(tc.tile_pool(name="reuse", bufs=1))
        psum = ctx.enter_context(tc.psum_pool(name="psum", bufs=1))

        def load_list(name, src):
            tile = keep.tile([P, S // GROUP], U16, name=name)
            nc.sync.dma_start(tile[:], src)
            return tile

        d_byte_table = keep.tile([P, G], U8)
        x_byte_table = keep.tile([P, T], U8)
        nc.vector.memset(d_byte_table[:].bitcast(I32), 0)
        nc.vector.memset(x_byte_table[:].bitcast(I32), 0)
        first_scales = keep.tile([P, H + S], U8, align_bytes=64)
        cand_scales = keep.tile([P, C], U8, align_bytes=64)
        nc.vector.memset(first_scales[:].bitcast(I32), 0)
        nc.vector.memset(cand_scales[:].bitcast(I32), 0)
        k1_list = load_list("k1_list", k1)
        offs_list = load_list("offs_list", offs)
        gains = reuse.tile([P, 16], F32, offset=PB_AT[1] - 32)
        gain, h_gain = gains[:, 0:PACK], gains[:, 8 : 8 + PACK]
        nc.gpsimd.dma_start(out=gain, in_=gs.rearrange("(p t) o -> p (t o)", t=PACK))
        cand_list = load_list("cand_list", cand)
        n1_list = load_list("n1_list", n1)
        nc.sync.dma_start(out=d_byte_table[0:P:8, :].bitcast(I32), in_=d_scales[0].bitcast(I32))
        nc.sync.dma_start(out=x_byte_table[0:P:8, :].bitcast(I32), in_=x_scales[0].bitcast(I32))
        x_word_table = keep.tile([P, T], I32)
        d_word_table = keep.tile([P, G], I32)
        nc.sync.dma_start(out=x_word_table[:], in_=x_words[0].rearrange("p n t -> p (n t)").bitcast(I32))
        nc.sync.dma_start(out=d_word_table[:], in_=d_words[0].rearrange("p n t -> p (n t)").bitcast(I32))
        n2_list = load_list("n2_list", n2)
        n3_list = load_list("n3_list", n3)
        n4_list = load_list("n4_list", n4)

        nc.scalar.activation(h_gain, gain, COPY, scale=0.0625)

        first_bytes = reuse.tile([P, H + S], U8, offset=0)
        nc.vector.tensor_copy(first_bytes[:, 0:H], d_byte_table[:].indirect(k1_list[:]))
        nc.vector.tensor_copy(first_bytes[:, H:], x_byte_table[:].indirect(offs_list[:]))
        place_scale_rows((nc.sync,), first_scales, first_bytes)

        xq_words = keep.tile([P, S], U32, align_bytes=64)
        nc.vector.tensor_copy(xq_words[:], x_word_table[:].bitcast(U32).indirect(offs_list[:]))
        dq_picked = keep.tile([P, H], U32)
        nc.vector.tensor_copy(dq_picked[:], d_word_table[:].bitcast(U32).indirect(k1_list[:]))
        dq_words = keep.tile([P, H], U32, align_bytes=64)
        dq_scales = keep.tile([P, H], U8, align_bytes=64)
        deal(nc, dq_scales[:], first_scales[:, 0:H], 16)
        deal(nc, dq_words[:], dq_picked[:], 4)

        windows = [keep.tile([P, S if t == 0 else 2 * S], F32, name=f"window{t}") for t in range(PACK)]
        h_last = keep.tile([P, S], F32)
        h_plain = [windows[t][:, S:] for t in range(1, PACK)] + [h_last[:]]
        for t in range(PACK):
            rows = slice(t * P, (t + 1) * P)
            bank = psum.tile([P, S], F32, name=f"h_bank{t}", tag=f"bank{PACK + t}")
            nc.tensor.matmul_mx(out=bank[:], lhsT=dq_words[:, rows].bitcast(FP8X4), lhsT_scale=dq_scales[:, rows],
                                rhs=xq_words[:].bitcast(FP8X4), rhs_scale=first_scales[:, H:], start=True, stop=True)
            nc.scalar.activation(windows[t][:, 0:S], bank[:], COPY, scale=h_gain[:, t : t + 1])
            nc.scalar.activation(h_plain[t], bank[:], COPY, scale=h_gain[:, t : t + 1])

        cand_bytes = reuse.tile([P, C], U8, offset=0)
        cand_dealt = keep.tile([P, C], U8)
        cand_words = reuse.tile([P, C], U32, align_bytes=64, offset=C)
        nc.vector.tensor_copy(cand_bytes[:], x_byte_table[:].indirect(cand_list[:]))
        nc.vector.tensor_copy(cand_words[:].rearrange("p (t m) -> p m t", t=PACK), x_word_table[:].bitcast(U32).indirect(cand_list[:]))
        deal(nc, cand_dealt[:], cand_bytes[:], 16)
        place_scale_rows((nc.sync,), cand_scales, cand_dealt)

        minus_pa = keep.tile([P, PACK, S], F32)
        for t in range(PACK):
            for lo, hi in HALVES if t == 0 else WHOLE:
                nc.vector.tensor_tensor(minus_pa[:, t, lo:hi], windows[t][:].indirect(entries(n1_list, lo, hi)), h_plain[t][:, lo:hi], ALU.subtract)
        pa16, pb16 = [], []
        for lo, hi in HALVES:
            tile = keep.tile([P, hi - lo, PACK], BF16, name=f"pa16_{lo}")
            interleave(nc, tile[:], minus_pa[:, :, lo:hi], -1.0)
            pa16.append(tile[:].rearrange("p n t -> p (n t)"))
        for (lo, hi), at in zip(HALVES, PB_AT):
            pb = reuse.tile([P, PACK, hi - lo], F32, name=f"pb{lo}", offset=at)
            for t in range(PACK):
                nc.vector.tensor_tensor(pb[:, t, :], windows[t][:].indirect(entries(n2_list, lo, hi)), h_plain[t][:, lo:hi], ALU.subtract)
            tile = keep.tile([P, hi - lo, PACK], BF16, name=f"pb16_{lo}")
            interleave(nc, tile[:], pb[:], 1.0)
            pb16.append(tile[:].rearrange("p n t -> p (n t)"))

        s_plain = [keep.tile([P, S], F32, name=f"s_plain{t}") for t in range(PACK)]
        last_bank = psum.tile([P, S], F32)
        for half, (lo, hi) in enumerate(HALVES):
            n = PACK * (hi - lo)
            s_banks = [psum.tile([P, hi - lo], F32, name=f"s_bank{half}_{t}", tag=f"bank{PACK * half + t}")[:] for t in range(PACK - 1)]
            s_banks.append(last_bank[:, lo:hi])
            upper = keep.tile([P, n], BF16, name=f"upper{lo}")
            lower = keep.tile([P, n], BF16, name=f"lower{lo}")
            capped = keep.tile([P, n], BF16, name=f"capped{lo}")
            z = keep.tile([P, n], BF16, name=f"z{lo}", align_bytes=64)
            nc.vector.tensor_scalar(upper[:], pb16[half], 0.0, None, ALU.max)
            nc.vector.tensor_scalar(lower[:], pb16[half], 0.0, None, ALU.min)
            parts = [slice(PACK * c, PACK * (c + QUARTER)) for c in range(0, hi - lo, QUARTER)]
            for part in parts:
                nc.vector.tensor_tensor(capped[:, part], pa16[half][:, part], upper[:, part], ALU.min)
            for part in parts:
                nc.vector.tensor_tensor(z[:, part], capped[:, part], lower[:, part], ALU.max)
            for k, part in enumerate(parts):
                cols = slice(lo + k * QUARTER, lo + (k + 1) * QUARTER)
                z_words = keep.tile([P, QUARTER], U32, name=f"z_words{cols.start}", align_bytes=64)
                z_scales = keep.tile([P, QUARTER], U8, name=f"z_scales{cols.start}", align_bytes=64)
                nc.vector.quantize_mx(out=z_words[:].bitcast(FP8X4), scales=z_scales[:], in_=z[:, part])
                for t in range(PACK):
                    rows = slice(t * P, (t + 1) * P)
                    nc.tensor.matmul_mx(out=s_banks[t][:, k * QUARTER : (k + 1) * QUARTER], lhsT=cand_words[:, rows].bitcast(FP8X4), lhsT_scale=cand_scales[:, rows],
                                        rhs=z_words[:].bitcast(FP8X4), rhs_scale=z_scales[:], start=True, stop=True)
            for t in range(PACK - 1):
                nc.scalar.activation(windows[t][:, lo:hi], s_banks[t], COPY, scale=0.75 * 0.0625)
                nc.scalar.activation(s_plain[t][:, lo:hi], s_banks[t], COPY, scale=-0.0625)
        nc.scalar.activation(windows[PACK - 1][:, 0:S], last_bank[:], COPY, scale=0.75 * 0.0625)
        nc.scalar.activation(s_plain[PACK - 1][:], last_bank[:], COPY, scale=-0.0625)

        out_rows = out.rearrange("(p t) j -> p t j", t=PACK)

        def first_lookup(t):
            part = keep.tile([P, S], F32, name=f"part{t}")
            for lo, hi in HALVES if t == 0 else WHOLE:
                nc.vector.tensor_tensor(part[:, lo:hi], windows[t][:].indirect(entries(n3_list, lo, hi)), s_plain[t][:, lo:hi], ALU.add)
            return part

        def second_lookup(t, part):
            res = keep.tile([P, S], F32, name=f"res{t}")
            for lo, hi in HALVES if t in (0, PACK - 1) else WHOLE:
                nc.vector.tensor_tensor(res[:, lo:hi], windows[t][:].indirect(entries(n4_list, lo, hi)), part[:, lo:hi], ALU.add)
                nc.sync.dma_start(out=out_rows[:, t, lo:hi], in_=res[:, lo:hi])

        second_lookup(0, first_lookup(0))
        part = first_lookup(1)
        for t in range(1, PACK - 1):
            ahead = first_lookup(t + 1)
            second_lookup(t, part)
            part = ahead
        second_lookup(PACK - 1, part)
